import numpy as np, ml_dtypes
CORES = [83,85,87,115,117,119]
N = 6
import mx_ref
NC, G = 128, 2
C, C2 = np.float32(0.043), np.float32(0.01755)
BF = ml_dtypes.bfloat16
def cut(t, i, w=512):
    return t[:, w * i:w * i + w]
def tile(rs):
    return np.stack(rs, axis=2).reshape(128, -1).astype(BF)
def layer(w, X):
    out = []
    for i in range(G):
        for t in range(len(X)):
            p = mx_ref.matmul(mx_ref.quantize(cut(w, len(X) * i + t)), X[t])
            z = p if t == 0 else z + p
        out.append(z)
    return out
def act(Z):
    return [np.maximum(s * z, 0) * C for z in Z for s in (1, -1)]
def act2(Z):
    return [np.maximum(s * z, 0) * C2 for z in Z for s in (1, -1)]
def setup_inputs(rng):
    def f(*shape):
        return mx_ref.flush((rng.standard_normal(shape, dtype=np.float32) * np.exp2(rng.integers(-2, 3, shape[:-1] + (1,)))).astype(BF))
    return {"x": f(N, 128, 4 * NC), "w1": f(N, 128, G * 512), "w2": f(N, 128, G * 512), "w3": f(N, 128, G * 512), "w4": f(N, 128, 512)}
def setup_inputs_blocks(rng):
    d = setup_inputs(rng)
    for k in ("x", "w1", "w2", "w3", "w4"): d[k] = mx_ref.spread(d[k], rng, 2)
    return d
def setup_inputs_wide(rng):
    d = setup_inputs(rng)
    for k in ("x", "w1", "w2", "w3", "w4"): d[k] = mx_ref.flush((d[k].astype(np.float32) * np.exp2(rng.integers(-4, 5, (N, 1, 1))).astype(np.float32)).astype(BF))
    return d
def reference(x, w1, w2, w3, w4, own=None):
    X = [mx_ref.quantize(x[j]) for j in range(N)]
    t = np.stack([np.stack([tile(act(layer(w1[r], [X[c]]))) for c in range(N)]) for r in range(N)])
    uset = t if own is None else own["t"]
    h = np.zeros((N, 128, 4 * NC), BF)
    for c in range(N):
        for r in range(N):
            P = layer(w2[r], [mx_ref.quantize(uset[r][c])])
            Z = P if r == 0 else [z + p for z, p in zip(Z, P)]
        h[c] = tile(act2(Z))
    use = h if own is None else own["h"]
    H = [mx_ref.quantize(use[j]) for j in range(N)]
    y = np.zeros((N, 128, NC), np.float32)
    for c in range(N):
        for r in range(N):
            p = mx_ref.matmul(mx_ref.quantize(w4[r]), mx_ref.quantize(tile(act(layer(w3[r], [H[c]])))))
            y[c] = p if r == 0 else y[c] + p
    return {"t": t, "h": h, "y": y}

@@ -1,0 +1,354 @@
+from concourse.bass import DstId, RemoteDMATransfer
+from concourse.mybir import dt, AluOpType, ActivationFunctionType as AF
+
+N = 6
+K = 128
+C1, C2 = 0.043, 0.01755
+F8 = "float8_e4m3fn_x4"
+
+SCRATCH = {
+    "xb": ("sbuf", [128, 512], "bfloat16"),
+    "w1b": ("sbuf", [128, 1024], "bfloat16"),
+    "w2b": ("sbuf", [128, 1024], "bfloat16"),
+    "w3b": ("sbuf", [128, 1024], "bfloat16"),
+    "w4b": ("sbuf", [128, 512], "bfloat16"),
+    "xq": ("sbuf", [128, N * K], F8), "xs": ("sbuf", [128, N * K], "uint8"),
+    "w1q": ("sbuf", [128, 2 * K], F8), "w1s": ("sbuf", [128, 2 * K], "uint8"),
+    "w2q": ("sbuf", [128, 2 * K], F8), "w2s": ("sbuf", [128, 2 * K], "uint8"),
+    "wq": ("sbuf", [128, N * 3 * K], F8), "ws": ("sbuf", [128, N * 3 * K], "uint8"),
+    "tq": ("sbuf", [128, N * K], F8), "ts": ("sbuf", [128, N * K], "uint8"),
+    "hq": ("sbuf", [128, K], F8), "hs": ("sbuf", [128, K], "uint8"),
+    "uq": ("sbuf", [128, N * K], F8), "us": ("sbuf", [128, N * K], "uint8"),
+    "rq": ("sbuf", [128, 3 * K], F8), "rs": ("sbuf", [128, 3 * K], "uint8"),
+    "tb": ("sbuf", [128, N * 512], "bfloat16"),
+    "hb": ("sbuf", [128, 512], "bfloat16"),
+    "ub": ("sbuf", [128, N * 512], "bfloat16"),
+    "pf": ("sbuf", [128, N * 256], "float32"),
+    "lc": ("sbuf", [128, 3 * 256], "float32"),
+    "lo": ("sbuf", [128, 3 * 256], "float32"),
+    "so": ("sbuf", [128, 256], "float32"),
+    "sx": ("sbuf", [128, 256], "float32"),
+    "tmp": ("sbuf", [128, 256], "float32"),
+    "sm": ("sbuf", [128, 256], "float32"),
+    "yb": ("sbuf", [128, K], "float32"),
+    "ps": ("psum", [128, 8 * 512], "float32"),
+}
+SEMAPHORES = (["ldx", "ldw1", "ldw2", "ldw34", "qv", "qs", "qt", "sent", "go", "out", "so", "sx", "rp", "rc", "jc", "jo"]
+              + ["x%d" % i for i in range(N)] + ["w%d" % i for i in range(N)])
+
+
+def bits(m):
+    return bin(m).count("1")
+
+
+def rot(v, k):
+    k %= len(v)
+    return v[k:] + v[:k]
+
+
+def plan(T, topo):
+    teams = {}
+    for c in T.cores:
+        teams.setdefault(topo.chip(c), []).append(c)
+    other = {}
+    chips = sorted(teams)
+    other[chips[0]], other[chips[1]] = chips[1], chips[0]
+    relay, collect, local = {}, {}, {}
+    for ch in chips:
+        free = [c for c in range(topo.CHIPS * topo.CORES_PER_CHIP) if topo.chip(c) == ch and T.rank_of(c) is None]
+        far = teams[other[ch]]
+        d0 = topo.die(far[0])
+        a = [c for c in free if topo.die(c) == d0]
+        b = [c for c in free if topo.die(c) != d0]
+        relay.update(zip(far, (a[2], b[0], b[1])))
+        collect.update(zip(far, (a[0], a[1], b[0])))
+        local.update(zip(teams[ch], (a[0], a[1], b[1])))
+    return teams, other, relay, collect, local
+
+
+def rank_program(g, core, T, topo):
+    teams, other, relay, collect, local = plan(T, topo)
+    ch = topo.chip(core)
+    if ch not in teams:
+        return
+    here, far = teams[ch], teams[other[ch]]
+    on = topo.mask(core, [c for c in here if c != core][0])
+    off = topo.mask(core, far[0])
+    hi = on & ~off
+    sent = [0]
+
+    def xfer(dsts, outs, ins, mask, sem, fold=0):
+        sent[0] += bits(mask)
+        ids = []
+        for d in dsts:
+            rid, pid, _e = topo.addr(d)
+            ids.append(DstId(rid=rid, pnc=pid))
+        return RemoteDMATransfer(dst_ids=ids, dma_engine_mask=mask, remote_sem=T.sem[sem], srcs=ins, dsts=outs, alu_op=fold)
+
+    def send(*transfers):
+        g.remote_dma_fused(list(transfers), local_sem=T.sem.sent)
+
+    def codes(buf, a, b):
+        return buf[:, a:b].bitcast(dt.uint8)
+
+    def relay_mask(h):
+        return hi if h in collect.values() else on
+
+    rank = T.rank_of(core)
+    if rank is None:
+        for r in far:
+            if relay[r] == core:
+                i = T.rank_of(r)
+                dsts = rot(here, far.index(r))
+                a, b = 3 * K * i, 3 * K * (i + 1)
+                g.wait_ge(T.sem.rp, bits(off))
+                send(xfer(dsts, [T.ws[:, a:b] for _d in dsts], [T.rs[:]], off, "w%d" % i))
+                g.wait_ge(T.sem.rc, bits(off))
+                send(xfer(dsts, [codes(T.wq, a, b) for _d in dsts], [codes(T.rq, 0, 3 * K)], relay_mask(core), "w%d" % i))
+        for c in here:
+            if local[c] == core:
+                src = [T.lo[:, 256 * k:256 * k + 256] for k in range(3) if here[k] != c]
+                g.wait_ge(T.sem.jo, bits(off) + bits(hi))
+                send(xfer([c], [T.so[:]], src, off, "so", 1))
+        for c in far:
+            if collect[c] == core:
+                g.wait_ge(T.sem.jc, 3 * bits(on))
+                send(xfer([c], [T.sx[:]], [T.lc[:, 256 * k:256 * k + 256] for k in range(3)], off, "sx", 1))
+        if sent[0]:
+            g.wait_ge(T.sem.sent, sent[0])
+        return
+
+    pos = here.index(core)
+    ten, vec, act, syn = g.tensor, g.vector, g.scalar, g.sync
+    queues = {"t": ten, "v": vec, "s": act, "y": syn, "g": g}
+    count = {"t": 0, "v": 0, "s": 0}
+    seen = {}
+
+    def done(q, ins):
+        count[q] += 1
+        ins.then_inc(T.sem["q" + q], 1)
+        return ("q" + q, count[q])
+
+    def need(q, *events):
+        for sem, val in events:
+            if seen.get((q, sem), 0) < val:
+                seen[(q, sem)] = val
+                queues[q].wait_ge(T.sem[sem], val)
+
+    syn.dma_start(T.xb[:], T.x[:]).then_inc(T.sem.ldx, 16)
+    act.dma_start(T.w1b[:], T.w1[:]).then_inc(T.sem.ldw1, 16)
+    syn.dma_start(T.w3b[:], T.w3[:]).then_inc(T.sem.ldw34, 16)
+    syn.dma_start(T.w4b[:], T.w4[:]).then_inc(T.sem.ldw34, 16)
+    act.dma_start(T.w2b[:], T.w2[:]).then_inc(T.sem.ldw2, 16)
+
+    own = 3 * K * rank
+    need("v", ("ldx", 16))
+    e_x = done("v", vec.quantize_mx(T.xq[:, K * rank:K * rank + K], T.xs[:, K * rank:K * rank + K], T.xb[:]))
+    need("v", ("ldw1", 16))
+    e_w1 = done("v", vec.quantize_mx(T.w1q[:], T.w1s[:], T.w1b[:]))
+
+    p_send = [here[(pos + k) % 3] for k in (1, 2)]
+    x_send = rot(far, pos)
+    p_recv = [here[(pos - k) % 3] for k in (1, 2)]
+    x_recv = [far[(pos - k) % 3] for k in range(3)]
+    order = [T.rank_of(c) for c in [core] + p_recv + x_recv]
+
+    xa, xz = K * rank, K * rank + K
+    need("g", e_x)
+    sx = "x%d" % rank
+    send(xfer(x_send, [T.xs[:, xa:xz]] * 3, [T.xs[:, xa:xz]], off, sx),
+         xfer(p_send, [T.xs[:, xa:xz]] * 2, [T.xs[:, xa:xz]], hi, sx))
+    send(xfer(x_send, [codes(T.xq, xa, xz)] * 3, [codes(T.xq, xa, xz)], off, sx),
+         xfer(p_send, [codes(T.xq, xa, xz)] * 2, [codes(T.xq, xa, xz)], hi, sx))
+
+    def x_ready(c):
+        if c == rank:
+            return e_x
+        m = hi if T.cores[c] in here else off
+        return ("x%d" % c, 2 * bits(m))
+
+    def w_ready(r):
+        if r == rank:
+            return e_w34
+        if T.cores[r] in here:
+            return ("w%d" % r, 2 * bits(hi))
+        return ("w%d" % r, bits(off) + bits(relay_mask(relay[T.cores[r]])))
+
+    free = {b: [] for b in range(8)}
+
+    def bank(b, n=K):
+        return T.ps[:, 512 * b:512 * b + n]
+
+    def mm(b, wq, ws, a, xq, xs, xa_, start=True, stop=True):
+        need("t", *free[b])
+        return done("t", ten.matmul_mx(bank(b), wq[:, a:a + K], ws[:, a:a + K], xq[:, xa_:xa_ + K], xs[:, xa_:xa_ + K], start, stop))
+
+    def out4(buf, slot, b):
+        return buf[:, 512 * slot + b:512 * slot + 512:4]
+
+    def relu_s(buf, slot, b, src, sign, c):
+        return done("s", act.activation(out4(buf, slot, b), src, AF.Relu, scale=sign * c))
+
+    def relu_v(buf, slot, b, src, sign, c):
+        if sign > 0:
+            return done("v", vec.tensor_scalar(out4(buf, slot, b), src, 0.0, c, AluOpType.max, AluOpType.mult))
+        return done("v", vec.tensor_scalar(out4(buf, slot, b), src, -c, 0.0, AluOpType.mult, AluOpType.max))
+
+    e_z, e_t, e_q, e_p, e_pt = {}, {}, {}, {}, {}
+
+    def z1(j):
+        c = order[j]
+        need("t", e_w1, x_ready(c))
+        e_z[j] = [mm(2 * (j % 2) + i, T.w1q, T.w1s, K * i, T.xq, T.xs, K * c) for i in range(2)]
+
+    def t1_s(j):
+        c, b = order[j], 2 * (j % 2)
+        need("s", e_z[j][0])
+        relu_s(T.tb, c, 0, bank(b), 1, C1)
+        e = relu_s(T.tb, c, 1, bank(b), -1, C1)
+        free[b] = [e]
+        e_t[j] = e
+
+    def t1_v(j):
+        c, b = order[j], 2 * (j % 2) + 1
+        need("v", e_z[j][1])
+        relu_v(T.tb, c, 2, bank(b), 1, C1)
+        e = relu_v(T.tb, c, 3, bank(b), -1, C1)
+        free[b] = [e]
+        need("v", e, e_t[j])
+        e_q[j] = done("v", vec.quantize_mx(T.tq[:, K * c:K * c + K], T.ts[:, K * c:K * c + K], T.tb[:, 512 * c:512 * c + 512]))
+
+    def p1(j):
+        c = order[j]
+        need("t", e_w2, e_q[j])
+        e_pt[j] = [mm(4 + 2 * (j % 2) + i, T.w2q, T.w2s, K * i, T.tq, T.ts, K * c) for i in range(2)]
+
+    def copy1(j):
+        c = order[j]
+        for i in range(2):
+            b = 4 + 2 * (j % 2) + i
+            need("s", e_pt[j][i])
+            e_p[j] = done("s", act.activation(T.pf[:, 256 * c + K * i:256 * c + K * i + K], bank(b), AF.Copy))
+            free[b] = [e_p[j]]
+
+    z1(0)
+    t1_s(0)
+    t1_v(0)
+    need("v", ("ldw34", 32))
+    vec_w3 = done("v", vec.quantize_mx(T.wq[:, own:own + 2 * K], T.ws[:, own:own + 2 * K], T.w3b[:]))
+    e_w34 = done("v", vec.quantize_mx(T.wq[:, own + 2 * K:own + 3 * K], T.ws[:, own + 2 * K:own + 3 * K], T.w4b[:]))
+    need("v", ("ldw2", 16))
+    e_w2 = done("v", vec.quantize_mx(T.w2q[:], T.w2s[:], T.w2b[:]))
+
+    wa, wz = own, own + 3 * K
+    sw = "w%d" % rank
+    need("g", vec_w3, e_w34)
+    send(xfer([relay[core]], [T.rs[:]], [T.ws[:, wa:wz]], off, "rp"),
+         xfer(p_send, [T.ws[:, wa:wz]] * 2, [T.ws[:, wa:wz]], hi, sw))
+    send(xfer([relay[core]], [codes(T.rq, 0, 3 * K)], [codes(T.wq, wa, wz)], off, "rc"),
+         xfer(p_send, [codes(T.wq, wa, wz)] * 2, [codes(T.wq, wa, wz)], hi, sw))
+
+    for first in (0, 3):
+        if first:
+            z1(3)
+            t1_s(3)
+            t1_v(3)
+        z1(first + 1)
+        t1_s(first + 1)
+        t1_v(first + 1)
+        p1(first)
+        copy1(first)
+        z1(first + 2)
+        t1_s(first + 2)
+        t1_v(first + 2)
+        p1(first + 1)
+        copy1(first + 1)
+        p1(first + 2)
+        copy1(first + 2)
+
+    mine = slice(256 * pos, 256 * pos + 256)
+    need("g", e_p[1], e_p[2])
+    send(*[xfer([local[c]], [T.lo[:, mine]], [T.pf[:, 256 * T.rank_of(c):256 * T.rank_of(c) + 256]], m, "jo")
+           for c, m in zip(p_send, rot([off, hi], 0))])
+    for j in (3, 4, 5):
+        c = order[j]
+        need("g", e_p[j])
+        send(xfer([collect[T.cores[c]]], [T.lc[:, mine]], [T.pf[:, 256 * c:256 * c + 256]], on, "jc"))
+    g.sem_inc(T.sem.go)
+
+    syn.wait_ge(T.sem.go, 1)
+    for j in range(N):
+        c = order[j]
+        need("y", e_t[j], e_q[j])
+        syn.dma_start(T.t[c], T.tb[:, 512 * c:512 * c + 512]).then_inc(T.sem.out, 16)
+
+    po = 256 * rank
+    need("v", e_p[0], ("so", bits(off)))
+    e_tmp = done("v", vec.tensor_tensor(T.tmp[:], T.pf[:, po:po + 256], T.so[:], AluOpType.add))
+    need("v", e_tmp, ("sx", bits(off)))
+    e_s = [done("v", vec.tensor_tensor(T.sm[:, K * i:K * i + K], T.tmp[:, K * i:K * i + K], T.sx[:, K * i:K * i + K], AluOpType.add))
+           for i in range(2)]
+    need("s", e_s[0])
+    relu_s(T.hb, 0, 0, T.sm[:, 0:K], 1, C2)
+    relu_s(T.hb, 0, 1, T.sm[:, 0:K], -1, C2)
+    need("s", e_s[1])
+    e_hs = relu_s(T.hb, 0, 2, T.sm[:, K:2 * K], 1, C2)
+    need("v", e_s[1])
+    e_hv = relu_v(T.hb, 0, 3, T.sm[:, K:2 * K], -1, C2)
+    need("v", e_hs, e_hv)
+    e_h = done("v", vec.quantize_mx(T.hq[:], T.hs[:], T.hb[:]))
+    need("y", e_hs, e_hv)
+    syn.dma_start(T.h[:], T.hb[:]).then_inc(T.sem.out, 16)
+
+    sets = [(0, 1), (2, 3), (4, 5)]
+    YB = 6
+
+    def z2(j):
+        r = order[j]
+        need("t", e_h, w_ready(r))
+        e_z[j] = [mm(sets[j % 3][i], T.wq, T.ws, 3 * K * r + K * i, T.hq, T.hs, 0) for i in range(2)]
+
+    def u2(j):
+        r = order[j]
+        b0, b1 = sets[j % 3]
+        need("s", e_z[j][0])
+        relu_s(T.ub, r, 0, bank(b0), 1, C1)
+        e = relu_s(T.ub, r, 1, bank(b0), -1, C1)
+        free[b0] = [e]
+        if j in (1, 3):
+            need("s", e_z[j][1])
+            relu_s(T.ub, r, 2, bank(b1), 1, C1)
+            e = relu_s(T.ub, r, 3, bank(b1), -1, C1)
+            free[b1] = [e]
+        else:
+            need("v", e_z[j][1])
+            relu_v(T.ub, r, 2, bank(b1), 1, C1)
+            ev = relu_v(T.ub, r, 3, bank(b1), -1, C1)
+            free[b1] = [ev]
+            need("v", ev)
+        need("v", e)
+        e_q[j] = done("v", vec.quantize_mx(T.uq[:, K * r:K * r + K], T.us[:, K * r:K * r + K], T.ub[:, 512 * r:512 * r + 512]))
+
+    def y2(j):
+        r = order[j]
+        need("t", e_q[j])
+        return mm(YB, T.wq, T.ws, 3 * K * r + 2 * K, T.uq, T.us, K * r, j == 0, j == N - 1)
+
+    z2(0)
+    z2(1)
+    u2(0)
+    u2(1)
+    for j in range(N):
+        if j + 2 < N:
+            z2(j + 2)
+            u2(j + 2)
+        e_y = y2(j)
+    need("v", e_y)
+    e_o = done("v", vec.tensor_copy(T.yb[:], bank(YB)))
+    need("y", e_o)
+    syn.dma_start(T.y[:], T.yb[:]).then_inc(T.sem.out, 16)
+
+    g.wait_ge(T.sem.sent, sent[0])
+    for q in ("s", "t", "v"):
+        need("g", ("q" + q, count[q]))
+    g.wait_ge(T.sem.out, 16 * (N + 2))

@@ -3,6 +3,7 @@ from concourse.mybir import dt, AluOpType, ActivationFunctionType as AF
 
 N = 6
 K = 128
+HW = 192
 C1, C2 = 0.043, 0.01755
 F8 = "float8_e4m3fn_x4"
 
@@ -19,13 +20,16 @@ SCRATCH = {
     "tq": ("sbuf", [128, N * K], F8), "ts": ("sbuf", [128, N * K], "uint8"),
     "hq": ("sbuf", [128, K], F8), "hs": ("sbuf", [128, K], "uint8"),
     "uq": ("sbuf", [128, N * K], F8), "us": ("sbuf", [128, N * K], "uint8"),
-    "rq": ("sbuf", [128, 3 * K], F8), "rs": ("sbuf", [128, 3 * K], "uint8"),
+    "rq": ("sbuf", [128, 2 * HW], F8), "rs": ("sbuf", [128, 2 * HW], "uint8"),
     "tb": ("sbuf", [128, N * 512], "bfloat16"),
     "hb": ("sbuf", [128, 512], "bfloat16"),
     "ub": ("sbuf", [128, N * 512], "bfloat16"),
     "pf": ("sbuf", [128, N * 256], "float32"),
-    "lc": ("sbuf", [128, 3 * 256], "float32"),
+    "lc": ("sbuf", [128, 2 * 3 * K], "float32"),
+    "ad": ("sbuf", [128, 2 * K], "float32"),
+    "ae": ("sbuf", [128, 2 * K], "float32"),
     "lo": ("sbuf", [128, 3 * 256], "float32"),
+    "nd": ("sbuf", [128, 256], "float32"),
     "so": ("sbuf", [128, 256], "float32"),
     "sx": ("sbuf", [128, 256], "float32"),
     "tmp": ("sbuf", [128, 256], "float32"),
@@ -33,12 +37,19 @@ SCRATCH = {
     "yb": ("sbuf", [128, K], "float32"),
     "ps": ("psum", [128, 8 * 512], "float32"),
 }
-SEMAPHORES = (["ldx", "ldw1", "ldw2", "ldw34", "qv", "qs", "qt", "sent", "go", "out", "so", "sx", "rp", "rc", "jc", "jo"]
+SEMAPHORES = (["ldx", "ldw1", "ldw2", "ldw34", "qv", "qs", "qt", "sent", "go", "out", "so", "sx0", "sx1",
+               "rp0", "rc0", "rp1", "rc1", "jo", "jn", "ja", "jf", "e0", "l0", "e1", "l1"]
               + ["x%d" % i for i in range(N)] + ["w%d" % i for i in range(N)])
 
 
 def bits(m):
     return bin(m).count("1")
+
+
+def halves(m):
+    b = [e for e in range(m.bit_length()) if m >> e & 1]
+    n = len(b) // 2
+    return [sum(1 << e for e in b[:n]), sum(1 << e for e in b[n:])]
 
 
 def rot(v, k):
@@ -60,9 +71,17 @@ def plan(T, topo):
         d0 = topo.die(far[0])
         a = [c for c in free if topo.die(c) == d0]
         b = [c for c in free if topo.die(c) != d0]
-        relay.update(zip(far, (a[2], b[0], b[1])))
-        collect.update(zip(far, (a[0], a[1], b[0])))
-        local.update(zip(teams[ch], (a[0], a[1], b[1])))
+
+        def deal(table, to):
+            held = []
+            for c, pair in zip(far, table):
+                for i, h in enumerate(pair):
+                    to[c, i] = (h, held.count(h))
+                    held.append(h)
+
+        deal(((a[0], b[0]), (a[1], b[1]), (a[2], a[0])), relay)
+        deal(((a[0], b[0]), (a[1], b[1]), (a[2], b[1])), collect)
+        local.update(zip(teams[ch], (a[1], a[2], b[0])))
     return teams, other, relay, collect, local
 
 
@@ -75,6 +94,7 @@ def rank_program(g, core, T, topo):
     on = topo.mask(core, [c for c in here if c != core][0])
     off = topo.mask(core, far[0])
     hi = on & ~off
+    half = (off, hi)
     sent = [0]
 
     def xfer(dsts, outs, ins, mask, sem, fold=0):
@@ -91,31 +111,56 @@ def rank_program(g, core, T, topo):
     def codes(buf, a, b):
         return buf[:, a:b].bitcast(dt.uint8)
 
-    def relay_mask(h):
-        return hi if h in collect.values() else on
-
     rank = T.rank_of(core)
     if rank is None:
-        for r in far:
-            if relay[r] == core:
-                i = T.rank_of(r)
-                dsts = rot(here, far.index(r))
-                a, b = 3 * K * i, 3 * K * (i + 1)
-                g.wait_ge(T.sem.rp, bits(off))
-                send(xfer(dsts, [T.ws[:, a:b] for _d in dsts], [T.rs[:]], off, "w%d" % i))
-                g.wait_ge(T.sem.rc, bits(off))
-                send(xfer(dsts, [codes(T.wq, a, b) for _d in dsts], [codes(T.rq, 0, 3 * K)], relay_mask(core), "w%d" % i))
+        vec = g.vector
+        pieces = sorted((relay[r, p][1], k, p) for k, r in enumerate(far) for p in range(2) if relay[r, p][0] == core)
+        work = sorted((collect[c, i][1], k, i) for k, c in enumerate(far) for i in range(2) if collect[c, i][0] == core)
+
+        for n, k, p in pieces:
+            i, dsts = T.rank_of(far[k]), rot(here, k)
+            a = 3 * K * i + HW * p
+            g.wait_ge(T.sem["rp%d" % n], bits(off) // 2)
+            send(xfer(dsts, [T.ws[:, a:a + HW] for _d in dsts], [T.rs[:, HW * n:HW * n + HW]], off, "w%d" % i))
+
         for c in here:
             if local[c] == core:
                 src = [T.lo[:, 256 * k:256 * k + 256] for k in range(3) if here[k] != c]
-                g.wait_ge(T.sem.jo, bits(off) + bits(hi))
-                send(xfer([c], [T.so[:]], src, off, "so", 1))
-        for c in far:
-            if collect[c] == core:
-                g.wait_ge(T.sem.jc, 3 * bits(on))
-                send(xfer([c], [T.sx[:]], [T.lc[:, 256 * k:256 * k + 256] for k in range(3)], off, "sx", 1))
-        if sent[0]:
-            g.wait_ge(T.sem.sent, sent[0])
+                vec.wait_ge(T.sem.jo, bits(off) + bits(hi))
+                vec.tensor_tensor(T.nd[:], src[0], src[1], AluOpType.add).then_inc(T.sem.jn, 1)
+                g.wait_ge(T.sem.jn, 1)
+                send(xfer([c], [T.so[:]], [T.nd[:]], hi, "so"))
+
+        def landed(job, p):
+            return T.lc[:, K * (3 * job + p):K * (3 * job + p) + K]
+
+        def last(k):
+            return (k + 2) % 3
+
+        for job, k, i in work:
+            early = [landed(job, p) for p in range(3) if p != last(k)]
+            vec.wait_ge(T.sem["e%d" % job], 2 * bits(half[i]))
+            vec.tensor_tensor(T.ad[:, K * job:K * job + K], early[0], early[1], AluOpType.add).then_inc(T.sem.ja, 1)
+        for n, (job, k, i) in enumerate(work):
+            src = [T.ad[:, K * job:K * job + K], landed(job, last(k))]
+            if len(work) > 1:
+                if n == 0:
+                    vec.wait_ge(T.sem.ja, len(work))
+                vec.wait_ge(T.sem["l%d" % job], bits(half[i]))
+                vec.tensor_tensor(T.ae[:, K * job:K * job + K], src[0], src[1], AluOpType.add).then_inc(T.sem.jf, 1)
+                g.wait_ge(T.sem.jf, n + 1)
+                send(xfer([far[k]], [T.sx[:, K * i:K * i + K]], [T.ae[:, K * job:K * job + K]], off, "sx%d" % i))
+            else:
+                g.wait_ge(T.sem.ja, 1)
+                g.wait_ge(T.sem["l%d" % job], bits(half[i]))
+                send(xfer([far[k]], [T.sx[:, K * i:K * i + K]], src, off, "sx%d" % i, 1))
+
+        for n, k, p in pieces:
+            i, dsts = T.rank_of(far[k]), rot(here, k)
+            a = 3 * K * i + HW * p
+            g.wait_ge(T.sem["rc%d" % n], bits(off) // 2)
+            send(xfer(dsts, [codes(T.wq, a, a + HW) for _d in dsts], [codes(T.rq, HW * n, HW * n + HW)], on, "w%d" % i))
+        g.wait_ge(T.sem.sent, sent[0])
         return
 
     pos = here.index(core)
@@ -130,21 +175,27 @@ def rank_program(g, core, T, topo):
         return ("q" + q, count[q])
 
     def need(q, *events):
+        best = {}
         for sem, val in events:
+            best[sem] = max(val, best.get(sem, 0))
+        for sem, val in best.items():
             if seen.get((q, sem), 0) < val:
                 seen[(q, sem)] = val
                 queues[q].wait_ge(T.sem[sem], val)
 
-    syn.dma_start(T.xb[:], T.x[:]).then_inc(T.sem.ldx, 16)
-    act.dma_start(T.w1b[:], T.w1[:]).then_inc(T.sem.ldw1, 16)
+    syn.dma_start(T.xb[:, 0:256], T.x[:, 0:256]).then_inc(T.sem.ldx, 16)
+    act.dma_start(T.xb[:, 256:512], T.x[:, 256:512]).then_inc(T.sem.ldx, 16)
+    syn.dma_start(T.w1b[:, 0:512], T.w1[:, 0:512]).then_inc(T.sem.ldw1, 16)
+    act.dma_start(T.w1b[:, 512:1024], T.w1[:, 512:1024]).then_inc(T.sem.ldw1, 16)
     syn.dma_start(T.w3b[:], T.w3[:]).then_inc(T.sem.ldw34, 16)
-    syn.dma_start(T.w4b[:], T.w4[:]).then_inc(T.sem.ldw34, 16)
+    act.dma_start(T.w4b[:], T.w4[:]).then_inc(T.sem.ldw34, 16)
     act.dma_start(T.w2b[:], T.w2[:]).then_inc(T.sem.ldw2, 16)
 
     own = 3 * K * rank
-    need("v", ("ldx", 16))
-    e_x = done("v", vec.quantize_mx(T.xq[:, K * rank:K * rank + K], T.xs[:, K * rank:K * rank + K], T.xb[:]))
-    need("v", ("ldw1", 16))
+    xa, xz = K * rank, K * rank + K
+    need("v", ("ldx", 32))
+    e_x = done("v", vec.quantize_mx(T.xq[:, xa:xz], T.xs[:, xa:xz], T.xb[:]))
+    need("v", ("ldw1", 32))
     e_w1 = done("v", vec.quantize_mx(T.w1q[:], T.w1s[:], T.w1b[:]))
 
     p_send = [here[(pos + k) % 3] for k in (1, 2)]
@@ -153,7 +204,6 @@ def rank_program(g, core, T, topo):
     x_recv = [far[(pos - k) % 3] for k in range(3)]
     order = [T.rank_of(c) for c in [core] + p_recv + x_recv]
 
-    xa, xz = K * rank, K * rank + K
     need("g", e_x)
     sx = "x%d" % rank
     send(xfer(x_send, [T.xs[:, xa:xz]] * 3, [T.xs[:, xa:xz]], off, sx),
@@ -164,15 +214,14 @@ def rank_program(g, core, T, topo):
     def x_ready(c):
         if c == rank:
             return e_x
-        m = hi if T.cores[c] in here else off
-        return ("x%d" % c, 2 * bits(m))
+        return ("x%d" % c, 2 * bits(hi if T.cores[c] in here else off))
 
     def w_ready(r):
         if r == rank:
             return e_w34
         if T.cores[r] in here:
-            return ("w%d" % r, 2 * bits(hi))
-        return ("w%d" % r, bits(off) + bits(relay_mask(relay[T.cores[r]])))
+            return ("w%d" % r, 2 * bits(on))
+        return ("w%d" % r, 2 * bits(off) + 2 * bits(on))
 
     free = {b: [] for b in range(8)}
 
@@ -196,98 +245,92 @@ def rank_program(g, core, T, topo):
 
     e_z, e_t, e_q, e_p, e_pt = {}, {}, {}, {}, {}
 
-    def z1(j):
-        c = order[j]
-        need("t", e_w1, x_ready(c))
-        e_z[j] = [mm(2 * (j % 2) + i, T.w1q, T.w1s, K * i, T.xq, T.xs, K * c) for i in range(2)]
-
-    def t1_s(j):
+    def t1(j):
         c, b = order[j], 2 * (j % 2)
+        need("t", e_w1, x_ready(c))
+        e_z[j] = [mm(b + i, T.w1q, T.w1s, K * i, T.xq, T.xs, K * c) for i in range(2)]
         need("s", e_z[j][0])
         relu_s(T.tb, c, 0, bank(b), 1, C1)
-        e = relu_s(T.tb, c, 1, bank(b), -1, C1)
-        free[b] = [e]
-        e_t[j] = e
-
-    def t1_v(j):
-        c, b = order[j], 2 * (j % 2) + 1
+        es = relu_s(T.tb, c, 1, bank(b), -1, C1)
         need("v", e_z[j][1])
-        relu_v(T.tb, c, 2, bank(b), 1, C1)
-        e = relu_v(T.tb, c, 3, bank(b), -1, C1)
-        free[b] = [e]
-        need("v", e, e_t[j])
+        relu_v(T.tb, c, 2, bank(b + 1), 1, C1)
+        ev = relu_v(T.tb, c, 3, bank(b + 1), -1, C1)
+        free[b], free[b + 1] = [es], [ev]
+        e_t[j] = [es, ev]
+        need("v", es, ev)
         e_q[j] = done("v", vec.quantize_mx(T.tq[:, K * c:K * c + K], T.ts[:, K * c:K * c + K], T.tb[:, 512 * c:512 * c + 512]))
 
     def p1(j):
-        c = order[j]
+        c, b = order[j], 4 + 2 * (j % 2)
         need("t", e_w2, e_q[j])
-        e_pt[j] = [mm(4 + 2 * (j % 2) + i, T.w2q, T.w2s, K * i, T.tq, T.ts, K * c) for i in range(2)]
-
-    def copy1(j):
-        c = order[j]
+        e_pt[j] = [mm(b + i, T.w2q, T.w2s, K * i, T.tq, T.ts, K * c) for i in range(2)]
+        e_p[j] = []
         for i in range(2):
-            b = 4 + 2 * (j % 2) + i
-            need("s", e_pt[j][i])
-            e_p[j] = done("s", act.activation(T.pf[:, 256 * c + K * i:256 * c + K * i + K], bank(b), AF.Copy))
-            free[b] = [e_p[j]]
+            dst = T.pf[:, 256 * c + K * i:256 * c + K * i + K]
+            if i and j == N - 1:
+                need("v", e_pt[j][i])
+                e = done("v", vec.tensor_copy(dst, bank(b + i)))
+            else:
+                need("s", e_pt[j][i])
+                e = done("s", act.activation(dst, bank(b + i), AF.Copy))
+            free[b + i] = [e]
+            e_p[j].append(e)
 
-    z1(0)
-    t1_s(0)
-    t1_v(0)
+    t1(0)
     need("v", ("ldw34", 32))
-    vec_w3 = done("v", vec.quantize_mx(T.wq[:, own:own + 2 * K], T.ws[:, own:own + 2 * K], T.w3b[:]))
+    e_w3 = done("v", vec.quantize_mx(T.wq[:, own:own + 2 * K], T.ws[:, own:own + 2 * K], T.w3b[:]))
     e_w34 = done("v", vec.quantize_mx(T.wq[:, own + 2 * K:own + 3 * K], T.ws[:, own + 2 * K:own + 3 * K], T.w4b[:]))
     need("v", ("ldw2", 16))
     e_w2 = done("v", vec.quantize_mx(T.w2q[:], T.w2s[:], T.w2b[:]))
 
-    wa, wz = own, own + 3 * K
-    sw = "w%d" % rank
-    need("g", vec_w3, e_w34)
-    send(xfer([relay[core]], [T.rs[:]], [T.ws[:, wa:wz]], off, "rp"),
-         xfer(p_send, [T.ws[:, wa:wz]] * 2, [T.ws[:, wa:wz]], hi, sw))
-    send(xfer([relay[core]], [codes(T.rq, 0, 3 * K)], [codes(T.wq, wa, wz)], off, "rc"),
-         xfer(p_send, [codes(T.wq, wa, wz)] * 2, [codes(T.wq, wa, wz)], hi, sw))
+    need("g", e_w3, e_w34)
+    ways = [(p, m) + relay[core, p] for p, m in enumerate(halves(off))]
+    send(*[xfer([h], [T.rs[:, HW * n:HW * n + HW]], [T.ws[:, own + HW * p:own + HW * p + HW]], m, "rp%d" % n) for p, m, h, n in ways])
+    send(*[xfer([h], [codes(T.rq, HW * n, HW * n + HW)], [codes(T.wq, own + HW * p, own + HW * p + HW)], m, "rc%d" % n)
+           for p, m, h, n in ways])
 
-    for first in (0, 3):
-        if first:
-            z1(3)
-            t1_s(3)
-            t1_v(3)
-        z1(first + 1)
-        t1_s(first + 1)
-        t1_v(first + 1)
-        p1(first)
-        copy1(first)
-        z1(first + 2)
-        t1_s(first + 2)
-        t1_v(first + 2)
-        p1(first + 1)
-        copy1(first + 1)
-        p1(first + 2)
-        copy1(first + 2)
+    t1(1)
+    for j in range(2, N):
+        t1(j)
+        p1(j - 1)
+    p1(N - 1)
+    p1(0)
 
     mine = slice(256 * pos, 256 * pos + 256)
-    need("g", e_p[1], e_p[2])
+    need("g", *(e_p[1] + e_p[2]))
     send(*[xfer([local[c]], [T.lo[:, mine]], [T.pf[:, 256 * T.rank_of(c):256 * T.rank_of(c) + 256]], m, "jo")
-           for c, m in zip(p_send, rot([off, hi], 0))])
+           for c, m in zip(p_send, half)])
     for j in (3, 4, 5):
         c = order[j]
-        need("g", e_p[j])
-        send(xfer([collect[T.cores[c]]], [T.lc[:, mine]], [T.pf[:, 256 * c:256 * c + 256]], on, "jc"))
+        need("g", *e_p[j])
+        parts = []
+        for i, m in enumerate(half):
+            to, job = collect[T.cores[c], i]
+            a = K * (3 * job + pos)
+            parts.append(xfer([to], [T.lc[:, a:a + K]], [T.pf[:, 256 * c + K * i:256 * c + K * i + K]], m,
+                              ("l%d" if j == 5 else "e%d") % job))
+        send(*parts)
+
+    sw = "w%d" % rank
+    send(xfer(p_send, [T.ws[:, own:own + 3 * K]] * 2, [T.ws[:, own:own + 3 * K]], on, sw))
+    send(xfer(p_send, [codes(T.wq, own, own + 3 * K)] * 2, [codes(T.wq, own, own + 3 * K)], on, sw))
     g.sem_inc(T.sem.go)
 
     syn.wait_ge(T.sem.go, 1)
     for j in range(N):
         c = order[j]
-        need("y", e_t[j], e_q[j])
+        need("y", *e_t[j])
         syn.dma_start(T.t[c], T.tb[:, 512 * c:512 * c + 512]).then_inc(T.sem.out, 16)
 
     po = 256 * rank
-    need("v", e_p[0], ("so", bits(off)))
+    need("v", *(e_p[0] + [("so", bits(hi))]))
     e_tmp = done("v", vec.tensor_tensor(T.tmp[:], T.pf[:, po:po + 256], T.so[:], AluOpType.add))
-    need("v", e_tmp, ("sx", bits(off)))
-    e_s = [done("v", vec.tensor_tensor(T.sm[:, K * i:K * i + K], T.tmp[:, K * i:K * i + K], T.sx[:, K * i:K * i + K], AluOpType.add))
-           for i in range(2)]
+    need("v", e_tmp)
+    e_s = []
+    for i in range(2):
+        need("v", ("sx%d" % i, bits(off)))
+        e_s.append(done("v", vec.tensor_tensor(T.sm[:, K * i:K * i + K], T.tmp[:, K * i:K * i + K], T.sx[:, K * i:K * i + K],
+                                               AluOpType.add)))
     need("s", e_s[0])
     relu_s(T.hb, 0, 0, T.sm[:, 0:K], 1, C2)
     relu_s(T.hb, 0, 1, T.sm[:, 0:K], -1, C2)
@@ -300,33 +343,32 @@ def rank_program(g, core, T, topo):
     need("y", e_hs, e_hv)
     syn.dma_start(T.h[:], T.hb[:]).then_inc(T.sem.out, 16)
 
-    sets = [(0, 1), (2, 3), (4, 5)]
     YB = 6
 
     def z2(j):
-        r = order[j]
+        r, b = order[j], 2 * (j % 3)
         need("t", e_h, w_ready(r))
-        e_z[j] = [mm(sets[j % 3][i], T.wq, T.ws, 3 * K * r + K * i, T.hq, T.hs, 0) for i in range(2)]
+        e_z[j] = [mm(b + i, T.wq, T.ws, 3 * K * r + K * i, T.hq, T.hs, 0) for i in range(2)]
 
     def u2(j):
-        r = order[j]
-        b0, b1 = sets[j % 3]
+        r, b = order[j], 2 * (j % 3)
         need("s", e_z[j][0])
-        relu_s(T.ub, r, 0, bank(b0), 1, C1)
-        e = relu_s(T.ub, r, 1, bank(b0), -1, C1)
-        free[b0] = [e]
-        if j in (1, 3):
+        relu_s(T.ub, r, 0, bank(b), 1, C1)
+        e0 = relu_s(T.ub, r, 1, bank(b), -1, C1)
+        if j in (0, 3):
             need("s", e_z[j][1])
-            relu_s(T.ub, r, 2, bank(b1), 1, C1)
-            e = relu_s(T.ub, r, 3, bank(b1), -1, C1)
-            free[b1] = [e]
+            relu_s(T.ub, r, 2, bank(b + 1), 1, C1)
+            e1 = relu_s(T.ub, r, 3, bank(b + 1), -1, C1)
         else:
             need("v", e_z[j][1])
-            relu_v(T.ub, r, 2, bank(b1), 1, C1)
-            ev = relu_v(T.ub, r, 3, bank(b1), -1, C1)
-            free[b1] = [ev]
-            need("v", ev)
-        need("v", e)
+            relu_v(T.ub, r, 2, bank(b + 1), 1, C1)
+            e1 = relu_v(T.ub, r, 3, bank(b + 1), -1, C1)
+        free[b], free[b + 1] = [e0], [e1]
+        e_t[j] = [e0, e1]
+
+    def q2(j):
+        r = order[j]
+        need("v", *e_t[j])
         e_q[j] = done("v", vec.quantize_mx(T.uq[:, K * r:K * r + K], T.us[:, K * r:K * r + K], T.ub[:, 512 * r:512 * r + 512]))
 
     def y2(j):
@@ -334,14 +376,15 @@ def rank_program(g, core, T, topo):
         need("t", e_q[j])
         return mm(YB, T.wq, T.ws, 3 * K * r + 2 * K, T.uq, T.us, K * r, j == 0, j == N - 1)
 
-    z2(0)
-    z2(1)
+    for j in range(3):
+        z2(j)
     u2(0)
-    u2(1)
     for j in range(N):
-        if j + 2 < N:
-            z2(j + 2)
-            u2(j + 2)
+        if j + 1 < N:
+            u2(j + 1)
+        if j + 3 < N:
+            z2(j + 3)
+        q2(j)
         e_y = y2(j)
     need("v", e_y)
     e_o = done("v", vec.tensor_copy(T.yb[:], bank(YB)))

from concourse.bass import DstId, RemoteDMATransfer
from concourse.mybir import dt, AluOpType, ActivationFunctionType as AF

N = 6
K = 128
HW = 192
C1, C2 = 0.043, 0.01755
F8 = "float8_e4m3fn_x4"

SCRATCH = {
    "xb": ("sbuf", [128, 512], "bfloat16"),
    "w1b": ("sbuf", [128, 1024], "bfloat16"),
    "w2b": ("sbuf", [128, 1024], "bfloat16"),
    "w3b": ("sbuf", [128, 1024], "bfloat16"),
    "w4b": ("sbuf", [128, 512], "bfloat16"),
    "xq": ("sbuf", [128, N * K], F8), "xs": ("sbuf", [128, N * K], "uint8"),
    "w1q": ("sbuf", [128, 2 * K], F8), "w1s": ("sbuf", [128, 2 * K], "uint8"),
    "w2q": ("sbuf", [128, 2 * K], F8), "w2s": ("sbuf", [128, 2 * K], "uint8"),
    "wq": ("sbuf", [128, N * 3 * K], F8), "ws": ("sbuf", [128, N * 3 * K], "uint8"),
    "tq": ("sbuf", [128, N * K], F8), "ts": ("sbuf", [128, N * K], "uint8"),
    "hq": ("sbuf", [128, K], F8), "hs": ("sbuf", [128, K], "uint8"),
    "uq": ("sbuf", [128, N * K], F8), "us": ("sbuf", [128, N * K], "uint8"),
    "rq": ("sbuf", [128, 2 * HW], F8), "rs": ("sbuf", [128, 2 * HW], "uint8"),
    "tb": ("sbuf", [128, N * 512], "bfloat16"),
    "hb": ("sbuf", [128, 512], "bfloat16"),
    "ub": ("sbuf", [128, N * 512], "bfloat16"),
    "pf": ("sbuf", [128, N * 256], "float32"),
    "lc": ("sbuf", [128, 2 * 3 * K], "float32"),
    "ad": ("sbuf", [128, 2 * K], "float32"),
    "ae": ("sbuf", [128, 2 * K], "float32"),
    "lo": ("sbuf", [128, 3 * 256], "float32"),
    "nd": ("sbuf", [128, 256], "float32"),
    "so": ("sbuf", [128, 256], "float32"),
    "sx": ("sbuf", [128, 256], "float32"),
    "tmp": ("sbuf", [128, 256], "float32"),
    "sm": ("sbuf", [128, 256], "float32"),
    "yb": ("sbuf", [128, K], "float32"),
    "ps": ("psum", [128, 8 * 512], "float32"),
}
SEMAPHORES = (["ldx", "ldw1", "ldw2", "ldw34", "qv", "qs", "qt", "sent", "go", "out", "so", "sx0", "sx1",
               "rp0", "rc0", "rp1", "rc1", "jo", "jn", "ja", "jf", "e0", "l0", "e1", "l1"]
              + ["x%d" % i for i in range(N)] + ["w%d" % i for i in range(N)])


def bits(m):
    return bin(m).count("1")


def halves(m):
    b = [e for e in range(m.bit_length()) if m >> e & 1]
    n = len(b) // 2
    return [sum(1 << e for e in b[:n]), sum(1 << e for e in b[n:])]


def rot(v, k):
    k %= len(v)
    return v[k:] + v[:k]


def plan(T, topo):
    teams = {}
    for c in T.cores:
        teams.setdefault(topo.chip(c), []).append(c)
    other = {}
    chips = sorted(teams)
    other[chips[0]], other[chips[1]] = chips[1], chips[0]
    relay, collect, local = {}, {}, {}
    for ch in chips:
        free = [c for c in range(topo.CHIPS * topo.CORES_PER_CHIP) if topo.chip(c) == ch and T.rank_of(c) is None]
        far = teams[other[ch]]
        d0 = topo.die(far[0])
        a = [c for c in free if topo.die(c) == d0]
        b = [c for c in free if topo.die(c) != d0]

        def deal(table, to):
            held = []
            for c, pair in zip(far, table):
                for i, h in enumerate(pair):
                    to[c, i] = (h, held.count(h))
                    held.append(h)

        deal(((a[0], b[0]), (a[1], b[1]), (a[2], a[0])), relay)
        deal(((a[0], b[0]), (a[1], b[1]), (a[2], b[1])), collect)
        local.update(zip(teams[ch], (a[1], a[2], b[0])))
    return teams, other, relay, collect, local


def rank_program(g, core, T, topo):
    teams, other, relay, collect, local = plan(T, topo)
    ch = topo.chip(core)
    if ch not in teams:
        return
    here, far = teams[ch], teams[other[ch]]
    on = topo.mask(core, [c for c in here if c != core][0])
    off = topo.mask(core, far[0])
    hi = on & ~off
    half = (off, hi)
    sent = [0]

    def xfer(dsts, outs, ins, mask, sem, fold=0):
        sent[0] += bits(mask)
        ids = []
        for d in dsts:
            rid, pid, _e = topo.addr(d)
            ids.append(DstId(rid=rid, pnc=pid))
        return RemoteDMATransfer(dst_ids=ids, dma_engine_mask=mask, remote_sem=T.sem[sem], srcs=ins, dsts=outs, alu_op=fold)

    def send(*transfers):
        g.remote_dma_fused(list(transfers), local_sem=T.sem.sent)

    def codes(buf, a, b):
        return buf[:, a:b].bitcast(dt.uint8)

    rank = T.rank_of(core)
    if rank is None:
        vec = g.vector
        pieces = sorted((relay[r, p][1], k, p) for k, r in enumerate(far) for p in range(2) if relay[r, p][0] == core)
        work = sorted((collect[c, i][1], k, i) for k, c in enumerate(far) for i in range(2) if collect[c, i][0] == core)

        for n, k, p in pieces:
            i, dsts = T.rank_of(far[k]), rot(here, k)
            a = 3 * K * i + HW * p
            g.wait_ge(T.sem["rp%d" % n], bits(off) // 2)
            send(xfer(dsts, [T.ws[:, a:a + HW] for _d in dsts], [T.rs[:, HW * n:HW * n + HW]], off, "w%d" % i))

        for c in here:
            if local[c] == core:
                src = [T.lo[:, 256 * k:256 * k + 256] for k in range(3) if here[k] != c]
                vec.wait_ge(T.sem.jo, bits(off) + bits(hi))
                vec.tensor_tensor(T.nd[:], src[0], src[1], AluOpType.add).then_inc(T.sem.jn, 1)
                g.wait_ge(T.sem.jn, 1)
                send(xfer([c], [T.so[:]], [T.nd[:]], hi, "so"))

        def landed(job, p):
            return T.lc[:, K * (3 * job + p):K * (3 * job + p) + K]

        def last(k):
            return (k + 2) % 3

        for job, k, i in work:
            early = [landed(job, p) for p in range(3) if p != last(k)]
            vec.wait_ge(T.sem["e%d" % job], 2 * bits(half[i]))
            vec.tensor_tensor(T.ad[:, K * job:K * job + K], early[0], early[1], AluOpType.add).then_inc(T.sem.ja, 1)
        for n, (job, k, i) in enumerate(work):
            src = [T.ad[:, K * job:K * job + K], landed(job, last(k))]
            if len(work) > 1:
                if n == 0:
                    vec.wait_ge(T.sem.ja, len(work))
                vec.wait_ge(T.sem["l%d" % job], bits(half[i]))
                vec.tensor_tensor(T.ae[:, K * job:K * job + K], src[0], src[1], AluOpType.add).then_inc(T.sem.jf, 1)
                g.wait_ge(T.sem.jf, n + 1)
                send(xfer([far[k]], [T.sx[:, K * i:K * i + K]], [T.ae[:, K * job:K * job + K]], off, "sx%d" % i))
            else:
                g.wait_ge(T.sem.ja, 1)
                g.wait_ge(T.sem["l%d" % job], bits(half[i]))
                send(xfer([far[k]], [T.sx[:, K * i:K * i + K]], src, off, "sx%d" % i, 1))

        for n, k, p in pieces:
            i, dsts = T.rank_of(far[k]), rot(here, k)
            a = 3 * K * i + HW * p
            g.wait_ge(T.sem["rc%d" % n], bits(off) // 2)
            send(xfer(dsts, [codes(T.wq, a, a + HW) for _d in dsts], [codes(T.rq, HW * n, HW * n + HW)], on, "w%d" % i))
        g.wait_ge(T.sem.sent, sent[0])
        return

    pos = here.index(core)
    ten, vec, act, syn = g.tensor, g.vector, g.scalar, g.sync
    queues = {"t": ten, "v": vec, "s": act, "y": syn, "g": g}
    count = {"t": 0, "v": 0, "s": 0}
    seen = {}

    def done(q, ins):
        count[q] += 1
        ins.then_inc(T.sem["q" + q], 1)
        return ("q" + q, count[q])

    def need(q, *events):
        best = {}
        for sem, val in events:
            best[sem] = max(val, best.get(sem, 0))
        for sem, val in best.items():
            if seen.get((q, sem), 0) < val:
                seen[(q, sem)] = val
                queues[q].wait_ge(T.sem[sem], val)

    syn.dma_start(T.xb[:, 0:256], T.x[:, 0:256]).then_inc(T.sem.ldx, 16)
    act.dma_start(T.xb[:, 256:512], T.x[:, 256:512]).then_inc(T.sem.ldx, 16)
    syn.dma_start(T.w1b[:, 0:512], T.w1[:, 0:512]).then_inc(T.sem.ldw1, 16)
    act.dma_start(T.w1b[:, 512:1024], T.w1[:, 512:1024]).then_inc(T.sem.ldw1, 16)
    syn.dma_start(T.w3b[:], T.w3[:]).then_inc(T.sem.ldw34, 16)
    act.dma_start(T.w4b[:], T.w4[:]).then_inc(T.sem.ldw34, 16)
    act.dma_start(T.w2b[:], T.w2[:]).then_inc(T.sem.ldw2, 16)

    own = 3 * K * rank
    xa, xz = K * rank, K * rank + K
    need("v", ("ldx", 32))
    e_x = done("v", vec.quantize_mx(T.xq[:, xa:xz], T.xs[:, xa:xz], T.xb[:]))
    need("v", ("ldw1", 32))
    e_w1 = done("v", vec.quantize_mx(T.w1q[:], T.w1s[:], T.w1b[:]))

    p_send = [here[(pos + k) % 3] for k in (1, 2)]
    x_send = rot(far, pos)
    p_recv = [here[(pos - k) % 3] for k in (1, 2)]
    x_recv = [far[(pos - k) % 3] for k in range(3)]
    order = [T.rank_of(c) for c in [core] + p_recv + x_recv]

    need("g", e_x)
    sx = "x%d" % rank
    send(xfer(x_send, [T.xs[:, xa:xz]] * 3, [T.xs[:, xa:xz]], off, sx),
         xfer(p_send, [T.xs[:, xa:xz]] * 2, [T.xs[:, xa:xz]], hi, sx))
    send(xfer(x_send, [codes(T.xq, xa, xz)] * 3, [codes(T.xq, xa, xz)], off, sx),
         xfer(p_send, [codes(T.xq, xa, xz)] * 2, [codes(T.xq, xa, xz)], hi, sx))

    def x_ready(c):
        if c == rank:
            return e_x
        return ("x%d" % c, 2 * bits(hi if T.cores[c] in here else off))

    def w_ready(r):
        if r == rank:
            return e_w34
        if T.cores[r] in here:
            return ("w%d" % r, 2 * bits(on))
        return ("w%d" % r, 2 * bits(off) + 2 * bits(on))

    free = {b: [] for b in range(8)}

    def bank(b, n=K):
        return T.ps[:, 512 * b:512 * b + n]

    def mm(b, wq, ws, a, xq, xs, xa_, start=True, stop=True):
        need("t", *free[b])
        return done("t", ten.matmul_mx(bank(b), wq[:, a:a + K], ws[:, a:a + K], xq[:, xa_:xa_ + K], xs[:, xa_:xa_ + K], start, stop))

    def out4(buf, slot, b):
        return buf[:, 512 * slot + b:512 * slot + 512:4]

    def relu_s(buf, slot, b, src, sign, c):
        return done("s", act.activation(out4(buf, slot, b), src, AF.Relu, scale=sign * c))

    def relu_v(buf, slot, b, src, sign, c):
        if sign > 0:
            return done("v", vec.tensor_scalar(out4(buf, slot, b), src, 0.0, c, AluOpType.max, AluOpType.mult))
        return done("v", vec.tensor_scalar(out4(buf, slot, b), src, -c, 0.0, AluOpType.mult, AluOpType.max))

    e_z, e_t, e_q, e_p, e_pt = {}, {}, {}, {}, {}

    def t1(j):
        c, b = order[j], 2 * (j % 2)
        need("t", e_w1, x_ready(c))
        e_z[j] = [mm(b + i, T.w1q, T.w1s, K * i, T.xq, T.xs, K * c) for i in range(2)]
        need("s", e_z[j][0])
        relu_s(T.tb, c, 0, bank(b), 1, C1)
        es = relu_s(T.tb, c, 1, bank(b), -1, C1)
        need("v", e_z[j][1])
        relu_v(T.tb, c, 2, bank(b + 1), 1, C1)
        ev = relu_v(T.tb, c, 3, bank(b + 1), -1, C1)
        free[b], free[b + 1] = [es], [ev]
        e_t[j] = [es, ev]
        need("v", es, ev)
        e_q[j] = done("v", vec.quantize_mx(T.tq[:, K * c:K * c + K], T.ts[:, K * c:K * c + K], T.tb[:, 512 * c:512 * c + 512]))

    def p1(j):
        c, b = order[j], 4 + 2 * (j % 2)
        need("t", e_w2, e_q[j])
        e_pt[j] = [mm(b + i, T.w2q, T.w2s, K * i, T.tq, T.ts, K * c) for i in range(2)]
        e_p[j] = []
        for i in range(2):
            dst = T.pf[:, 256 * c + K * i:256 * c + K * i + K]
            if i and j == N - 1:
                need("v", e_pt[j][i])
                e = done("v", vec.tensor_copy(dst, bank(b + i)))
            else:
                need("s", e_pt[j][i])
                e = done("s", act.activation(dst, bank(b + i), AF.Copy))
            free[b + i] = [e]
            e_p[j].append(e)

    t1(0)
    need("v", ("ldw34", 32))
    e_w3 = done("v", vec.quantize_mx(T.wq[:, own:own + 2 * K], T.ws[:, own:own + 2 * K], T.w3b[:]))
    e_w34 = done("v", vec.quantize_mx(T.wq[:, own + 2 * K:own + 3 * K], T.ws[:, own + 2 * K:own + 3 * K], T.w4b[:]))
    need("v", ("ldw2", 16))
    e_w2 = done("v", vec.quantize_mx(T.w2q[:], T.w2s[:], T.w2b[:]))

    need("g", e_w3, e_w34)
    ways = [(p, m) + relay[core, p] for p, m in enumerate(halves(off))]
    send(*[xfer([h], [T.rs[:, HW * n:HW * n + HW]], [T.ws[:, own + HW * p:own + HW * p + HW]], m, "rp%d" % n) for p, m, h, n in ways])
    send(*[xfer([h], [codes(T.rq, HW * n, HW * n + HW)], [codes(T.wq, own + HW * p, own + HW * p + HW)], m, "rc%d" % n)
           for p, m, h, n in ways])

    t1(1)
    for j in range(2, N):
        t1(j)
        p1(j - 1)
    p1(N - 1)
    p1(0)

    mine = slice(256 * pos, 256 * pos + 256)
    need("g", *(e_p[1] + e_p[2]))
    send(*[xfer([local[c]], [T.lo[:, mine]], [T.pf[:, 256 * T.rank_of(c):256 * T.rank_of(c) + 256]], m, "jo")
           for c, m in zip(p_send, half)])
    for j in (3, 4, 5):
        c = order[j]
        need("g", *e_p[j])
        parts = []
        for i, m in enumerate(half):
            to, job = collect[T.cores[c], i]
            a = K * (3 * job + pos)
            parts.append(xfer([to], [T.lc[:, a:a + K]], [T.pf[:, 256 * c + K * i:256 * c + K * i + K]], m,
                              ("l%d" if j == 5 else "e%d") % job))
        send(*parts)

    sw = "w%d" % rank
    send(xfer(p_send, [T.ws[:, own:own + 3 * K]] * 2, [T.ws[:, own:own + 3 * K]], on, sw))
    send(xfer(p_send, [codes(T.wq, own, own + 3 * K)] * 2, [codes(T.wq, own, own + 3 * K)], on, sw))
    g.sem_inc(T.sem.go)

    syn.wait_ge(T.sem.go, 1)
    for j in range(N):
        c = order[j]
        need("y", *e_t[j])
        syn.dma_start(T.t[c], T.tb[:, 512 * c:512 * c + 512]).then_inc(T.sem.out, 16)

    po = 256 * rank
    need("v", *(e_p[0] + [("so", bits(hi))]))
    e_tmp = done("v", vec.tensor_tensor(T.tmp[:], T.pf[:, po:po + 256], T.so[:], AluOpType.add))
    need("v", e_tmp)
    e_s = []
    for i in range(2):
        need("v", ("sx%d" % i, bits(off)))
        e_s.append(done("v", vec.tensor_tensor(T.sm[:, K * i:K * i + K], T.tmp[:, K * i:K * i + K], T.sx[:, K * i:K * i + K],
                                               AluOpType.add)))
    need("s", e_s[0])
    relu_s(T.hb, 0, 0, T.sm[:, 0:K], 1, C2)
    relu_s(T.hb, 0, 1, T.sm[:, 0:K], -1, C2)
    need("s", e_s[1])
    e_hs = relu_s(T.hb, 0, 2, T.sm[:, K:2 * K], 1, C2)
    need("v", e_s[1])
    e_hv = relu_v(T.hb, 0, 3, T.sm[:, K:2 * K], -1, C2)
    need("v", e_hs, e_hv)
    e_h = done("v", vec.quantize_mx(T.hq[:], T.hs[:], T.hb[:]))
    need("y", e_hs, e_hv)
    syn.dma_start(T.h[:], T.hb[:]).then_inc(T.sem.out, 16)

    YB = 6

    def z2(j):
        r, b = order[j], 2 * (j % 3)
        need("t", e_h, w_ready(r))
        e_z[j] = [mm(b + i, T.wq, T.ws, 3 * K * r + K * i, T.hq, T.hs, 0) for i in range(2)]

    def u2(j):
        r, b = order[j], 2 * (j % 3)
        need("s", e_z[j][0])
        relu_s(T.ub, r, 0, bank(b), 1, C1)
        e0 = relu_s(T.ub, r, 1, bank(b), -1, C1)
        if j in (0, 3):
            need("s", e_z[j][1])
            relu_s(T.ub, r, 2, bank(b + 1), 1, C1)
            e1 = relu_s(T.ub, r, 3, bank(b + 1), -1, C1)
        else:
            need("v", e_z[j][1])
            relu_v(T.ub, r, 2, bank(b + 1), 1, C1)
            e1 = relu_v(T.ub, r, 3, bank(b + 1), -1, C1)
        free[b], free[b + 1] = [e0], [e1]
        e_t[j] = [e0, e1]

    def q2(j):
        r = order[j]
        need("v", *e_t[j])
        e_q[j] = done("v", vec.quantize_mx(T.uq[:, K * r:K * r + K], T.us[:, K * r:K * r + K], T.ub[:, 512 * r:512 * r + 512]))

    def y2(j):
        r = order[j]
        need("t", e_q[j])
        return mm(YB, T.wq, T.ws, 3 * K * r + 2 * K, T.uq, T.us, K * r, j == 0, j == N - 1)

    for j in range(3):
        z2(j)
    u2(0)
    for j in range(N):
        if j + 1 < N:
            u2(j + 1)
        if j + 3 < N:
            z2(j + 3)
        q2(j)
        e_y = y2(j)
    need("v", e_y)
    e_o = done("v", vec.tensor_copy(T.yb[:], bank(YB)))
    need("y", e_o)
    syn.dma_start(T.y[:], T.yb[:]).then_inc(T.sem.out, 16)

    g.wait_ge(T.sem.sent, sent[0])
    for q in ("s", "t", "v"):
        need("g", ("q" + q, count[q]))
    g.wait_ge(T.sem.out, 16 * (N + 2))
